import numpy as np
import ml_dtypes


def mxq(x, axis, fmt="e4m3"):
    dtype, down = {"e4m3": (ml_dtypes.float8_e4m3fn, 7), "e5m2": (ml_dtypes.float8_e5m2, 14)}[fmt]
    v = np.moveaxis(np.asarray(x, np.float32).astype(ml_dtypes.bfloat16).astype(np.float64), axis, -1)
    blocks = v.reshape(v.shape[:-1] + (-1, 32))
    amax = np.abs(blocks).max(-1, keepdims=True)
    byte = np.maximum(np.where(amax > 0, np.frexp(amax)[1] - 1 + 127, 0) - down, 1)
    scale = np.exp2(byte - 127.0)
    codes = (blocks / scale).astype(np.float32).astype(dtype).astype(np.float64)
    return np.moveaxis((codes * scale).reshape(v.shape), -1, axis)


WIDE = False


def mx_kscale(k, group=512):
    if not WIDE:
        return np.ones(k)
    levels = np.array([10, -10, 5, -5, 0])
    if group != 512:
        return np.exp2(np.random.permutation(np.resize(levels, k // group))).repeat(group)
    if k % 512:
        return np.exp2(np.random.permutation(np.resize(levels, k // 32))).repeat(32)
    a = np.empty((k // 512, 16))
    for p in range(k // 512):
        a[p, :8] = np.random.permutation(np.resize(levels, 8))
        for g in range(8):
            far = levels[np.abs(levels - a[p, g]) >= 10]
            a[p, g + 8] = far[np.random.randint(len(far))]
    return np.exp2(a.ravel()).repeat(32)


def f64(x):
    return np.asarray(x).astype(np.float64)


def sigmoid(v):
    return 1.0 / (1.0 + np.exp(-v))


G, D, M, N = 2, 256, 128, 512


def setup_inputs():
    n = np.random.standard_normal
    s_d = mx_kscale(D, 0)
    return {
        "x": (n((G, D, N)) * s_d[:, None]).astype(np.float32),
        "w1": (n((G, D, M)) / np.sqrt(D) / s_d[:, None]).astype(np.float32),
        "w2": (n((G, D, M)) / np.sqrt(D) / s_d[:, None]).astype(np.float32),
        "w3": (n((G, D, M)) / np.sqrt(D) / s_d[:, None]).astype(np.float32),
        "dx": (n((G, D, N)) * s_d[:, None]).astype(np.float32),
        "og": (np.random.uniform(0.5, 2.0, (G, M, 1))).astype(np.float32),
        "base": (0.3 * n((G, M, N))).astype(np.float32),
    }


def reference(x, w1, w2, w3, dx, og, base):
    w1q = mxq(f64(w1), 1, "e4m3")
    xq = mxq(f64(x), 1, "e4m3")
    z1 = w1q.transpose(0, 2, 1) @ xq
    dxq = mxq(f64(dx), 1, "e4m3")
    tz1 = w1q.transpose(0, 2, 1) @ dxq
    w2q = mxq(f64(w2), 1, "e4m3")
    z2 = w2q.transpose(0, 2, 1) @ xq
    tz2 = w2q.transpose(0, 2, 1) @ dxq
    w3q = mxq(f64(w3), 1, "e4m3")
    z3 = w3q.transpose(0, 2, 1) @ xq
    tz3 = w3q.transpose(0, 2, 1) @ dxq
    sg = sigmoid(z1 * z2 + z3)
    xsg = (tz1 * z2 + tz2 * z1 + tz3) * sg * (1.0 - sg)
    xh = xsg * np.tanh(z3) + tz3 * (1.0 - np.square(np.tanh(z3))) * sg
    y = xh * f64(og) + f64(base)
    return y

@@ -1,0 +1,241 @@
+import concourse.mybir as mybir
+
+G, D, M, N = 2, 256, 128, 512
+FLOPS = 6 * 2 * G * D * M * N
+
+F32 = mybir.dt.float32
+BF16 = mybir.dt.bfloat16
+U32 = mybir.dt.uint32
+U8 = mybir.dt.uint8
+FP8X4 = mybir.dt.float8_e4m3fn_x4
+ALU = mybir.AluOpType
+ACT = mybir.ActivationFunctionType
+
+P = 128
+PACK = 4
+ROWS = D // PACK
+HALF = N // 2
+PIECE = 128
+
+
+def tile_rows_tnbilinsig_kernel(tc, x, w1, w2, w3, dx, og, base, out):
+    nc = tc.nc
+    with tc.tile_pool(name="sbuf", bufs=1) as sb, tc.psum_pool(name="psum", bufs=1) as ps, tc.manual_schedule():
+
+        def load_rows(name, src, c0, width):
+            raw = sb.tile([P, PACK, width], F32, name=name)
+            rows = src.rearrange("g (p j) n -> (g p) j n", j=PACK)
+            nc.sync.dma_start(out=raw[:], in_=rows[:, :, c0 : c0 + width])
+            return raw
+
+        def interleave(copy, grouped, g0, raw, c0, width):
+            copy(
+                out=grouped[:, g0 : g0 + width, :].rearrange("p (c i) j -> p c j i", i=4),
+                in_=raw[:, :, c0 : c0 + width].rearrange("p j (c i) -> p c j i", i=4),
+            )
+
+        def quantize(codes, scales, c0, grouped):
+            width = grouped.shape[1]
+            nc.vector.quantize_mx(
+                out=codes[:, c0 : c0 + width].bitcast(FP8X4),
+                scales=scales[:, c0 : c0 + width],
+                in_=grouped[:].rearrange("p c j -> p (c j)"),
+            )
+
+        def rounded(name, width):
+            return sb.tile([P, width, PACK], BF16, name=name, align_bytes=64)
+
+        w_codes = [sb.tile([P, M], U32, name="wc%d" % i, align_bytes=64) for i in range(3)]
+        w_scales = [sb.tile([P, M], U8, name="ws%d" % i, align_bytes=64) for i in range(3)]
+        x_codes = [sb.tile([P, N], U32, name="xc%d" % h, align_bytes=64) for h in range(2)]
+        x_scales = [sb.tile([P, N], U8, name="xs%d" % h, align_bytes=64) for h in range(2)]
+        banks = [[ps.tile([P, 2, HALF], F32, name="bank%d_%d" % (g, b)) for b in range(4)] for g in range(G)]
+
+        def bank(h, g, i):
+            return banks[g][(3 * h + i) % 4]
+
+        def product(h, g, i):
+            rows = slice(ROWS * g, ROWS * (g + 1))
+            nc.tensor.matmul_mx(
+                out=bank(h, g, i)[:].rearrange("p a n -> p (a n)"),
+                lhsT=w_codes[i][rows, :].bitcast(FP8X4),
+                lhsT_scale=w_scales[i][rows, :],
+                rhs=x_codes[h][rows, :].bitcast(FP8X4),
+                rhs_scale=x_scales[h][rows, :],
+                start=True,
+                stop=True,
+            )
+
+        vals = {}
+
+        def val(name, h, g, rows=1):
+            key = (name, h, g)
+            if key not in vals:
+                shape = [P, HALF] if rows == 1 else [P, rows, HALF]
+                vals[key] = sb.tile(shape, F32, name="%s%d%d" % key)
+            return vals[key]
+
+        def half_z1(h, g):
+            nc.scalar.activation(out=val("z1h", h, g)[:], in_=bank(h, g, 0)[:, 0, :], func=ACT.Copy, scale=0.5)
+
+        def half_z2(h, g):
+            nc.scalar.activation(out=val("z2h", h, g)[:], in_=bank(h, g, 1)[:, 0, :], func=ACT.Copy, scale=0.5)
+
+        def tanh_z3(h, g):
+            nc.scalar.activation(out=val("t", h, g)[:], in_=bank(h, g, 2)[:, 0, :], func=ACT.Tanh)
+
+        def square_t(h, g):
+            nc.scalar.activation(out=val("tt", h, g)[:], in_=val("t", h, g)[:], func=ACT.Square)
+
+        def tanh_a(h, g):
+            nc.scalar.activation(out=val("th", h, g)[:], in_=val("sums", h, g, 2)[:, 0, :], func=ACT.Tanh)
+
+        def step_a(h, g):
+            nc.vector.tensor_tensor(
+                out=val("prods", h, g, 2)[:],
+                in0=bank(h, g, 1)[:],
+                in1=val("z1h", h, g)[:].unsqueeze(1).to_broadcast([P, 2, HALF]),
+                op=ALU.mult,
+            )
+
+        def step_b(h, g):
+            nc.vector.tensor_tensor(out=val("m1", h, g)[:], in0=bank(h, g, 0)[:, 1, :], in1=val("z2h", h, g)[:], op=ALU.mult)
+
+        def step_c(h, g):
+            nc.vector.scalar_tensor_tensor(
+                out=val("sums", h, g, 2)[:], in0=bank(h, g, 2)[:], scalar=0.5, in1=val("prods", h, g, 2)[:],
+                op0=ALU.mult, op1=ALU.add,
+            )
+
+        def step_d(h, g):
+            nc.vector.scalar_tensor_tensor(
+                out=val("q", h, g)[:], in0=val("tt", h, g)[:], scalar=1.0, in1=bank(h, g, 2)[:, 1, :],
+                op0=ALU.subtract, op1=ALU.mult,
+            )
+
+        def step_sum(h, g):
+            nc.vector.tensor_tensor(out=val("b", h, g)[:], in0=val("m1", h, g)[:], in1=val("sums", h, g, 2)[:, 1, :], op=ALU.add)
+
+        def step_u(h, g):
+            nc.vector.scalar_tensor_tensor(
+                out=val("u", h, g)[:], in0=val("th", h, g)[:], scalar=1.0, in1=val("t", h, g)[:],
+                op0=ALU.subtract, op1=ALU.mult,
+            )
+
+        def step_r(h, g):
+            nc.vector.tensor_tensor(out=val("r", h, g)[:], in0=val("b", h, g)[:], in1=val("u", h, g)[:], op=ALU.mult)
+
+        def step_s(h, g):
+            nc.vector.tensor_tensor(out=val("s", h, g)[:], in0=val("r", h, g)[:], in1=val("q", h, g)[:], op=ALU.add)
+
+        def step_w(h, g):
+            nc.vector.scalar_tensor_tensor(
+                out=val("w", h, g)[:], in0=val("th", h, g)[:], scalar=1.0, in1=val("s", h, g)[:],
+                op0=ALU.add, op1=ALU.mult,
+            )
+
+        def step_y(h, g):
+            cols = slice(HALF * h, HALF * (h + 1))
+            nc.vector.scalar_tensor_tensor(
+                out=val("y", h, g)[:], in0=val("w", h, g)[:], scalar=gain[:, g : g + 1], in1=base_sb[g][:, cols],
+                op0=ALU.mult, op1=ALU.add,
+            )
+            nc.sync.dma_start(out=out[g, :, cols], in_=val("y", h, g)[:])
+
+        w1_raw = load_rows("w1_raw", w1, 0, M)
+        x0_raw = load_rows("x0_raw", x, 0, HALF)
+        dx0_raw = load_rows("dx0_raw", dx, 0, HALF)
+        w2_raw = load_rows("w2_raw", w2, 0, M)
+        w3_raw = load_rows("w3_raw", w3, 0, M)
+        x1_raw = load_rows("x1_raw", x, HALF, HALF)
+        dx1_raw = load_rows("dx1_raw", dx, HALF, HALF)
+        og_sb = sb.tile([P, G, 8], F32, name="og_sb")
+        with nc.allow_non_contiguous_dma(reason="one gain a partition"):
+            nc.sync.dma_start(out=og_sb[:, :, 0:1], in_=og.rearrange("g m o -> m g o"))
+        base_sb = [sb.tile([P, N], F32, name="base%d" % g) for g in range(G)]
+        for g in range(G):
+            nc.sync.dma_start(out=base_sb[g][:], in_=base[g])
+        gain = sb.tile([P, G], F32, name="gain")
+
+        w_bf = [rounded("wb%d" % i, M) for i in range(3)]
+        interleave(nc.vector.tensor_copy, w_bf[0], 0, w1_raw, 0, M)
+        quantize(w_codes[0], w_scales[0], 0, w_bf[0])
+        for name, raw, c0 in (("x0", x0_raw, 0), ("dx0", dx0_raw, HALF)):
+            lo = rounded(name + "lo", PIECE)
+            hi = rounded(name + "hi", PIECE)
+            interleave(nc.vector.tensor_copy, lo, 0, raw, 0, PIECE)
+            interleave(nc.scalar.copy, hi, 0, raw, PIECE, PIECE)
+            quantize(x_codes[0], x_scales[0], c0, lo)
+            quantize(x_codes[0], x_scales[0], c0 + PIECE, hi)
+        product(0, 0, 0)
+        interleave(nc.scalar.copy, w_bf[1], 0, w2_raw, 0, M)
+        quantize(w_codes[1], w_scales[1], 0, w_bf[1])
+        product(0, 0, 1)
+        product(0, 1, 0)
+        product(0, 1, 1)
+        interleave(nc.vector.tensor_copy, w_bf[2], 0, w3_raw, 0, M)
+
+        x1_bf = rounded("x1b", HALF)
+        dx1_bf = rounded("dx1b", HALF)
+
+        half_z1(0, 0)
+        step_a(0, 0)
+        quantize(w_codes[2], w_scales[2], 0, w_bf[2])
+        product(0, 0, 2)
+        product(0, 1, 2)
+        interleave(nc.scalar.copy, x1_bf, 0, x1_raw, 0, PIECE)
+        half_z2(0, 0)
+        half_z1(0, 1)
+        step_b(0, 0)
+        step_a(0, 1)
+        interleave(nc.scalar.copy, x1_bf, PIECE, x1_raw, PIECE, PIECE)
+        half_z2(0, 1)
+        step_c(0, 0)
+        step_b(0, 1)
+        step_c(0, 1)
+        quantize(x_codes[1], x_scales[1], 0, x1_bf)
+        for g in range(G):
+            tanh_z3(0, g)
+            tanh_a(0, g)
+            square_t(0, g)
+        interleave(nc.scalar.copy, dx1_bf, 0, dx1_raw, 0, PIECE)
+        interleave(nc.scalar.copy, dx1_bf, PIECE, dx1_raw, PIECE, PIECE)
+        nc.scalar.activation(out=gain[:], in_=og_sb[:, :, 0], func=ACT.Copy, scale=-0.5)
+        step_sum(0, 0)
+        step_sum(0, 1)
+        step_u(0, 0)
+        step_d(0, 0)
+        step_u(0, 1)
+        step_r(0, 0)
+        step_d(0, 1)
+        step_r(0, 1)
+        step_s(0, 0)
+        quantize(x_codes[1], x_scales[1], HALF, dx1_bf)
+        for g, i in ((0, 0), (0, 1), (1, 0), (1, 1), (0, 2), (1, 2)):
+            product(1, g, i)
+        step_s(0, 1)
+        for step in (step_w, step_y):
+            for g in range(G):
+                step(0, g)
+
+        for g in range(G):
+            half_z1(1, g)
+            half_z2(1, g)
+            step_a(1, g)
+            step_b(1, g)
+        for g in range(G):
+            tanh_z3(1, g)
+            step_c(1, g)
+        square_t(1, 0)
+        tanh_a(1, 0)
+        square_t(1, 1)
+        tanh_a(1, 1)
+        step_sum(1, 0)
+        step_sum(1, 1)
+        step_d(1, 0)
+        step_u(1, 0)
+        step_d(1, 1)
+        step_u(1, 1)
+        for step in (step_r, step_s, step_w, step_y):
+            for g in range(G):
+                step(1, g)

@@ -68,79 +68,98 @@ def tile_rows_tnbilinsig_kernel(tc, x, w1, w2, w3, dx, og, base, out):
 
         vals = {}
 
-        def val(name, h, g, rows=1):
-            key = (name, h, g)
+        def both(name, h, rows=1):
+            key = (name, h)
             if key not in vals:
-                shape = [P, HALF] if rows == 1 else [P, rows, HALF]
-                vals[key] = sb.tile(shape, F32, name="%s%d%d" % key)
+                shape = [P, G, HALF] if rows == 1 else [P, G, rows, HALF]
+                vals[key] = sb.tile(shape, F32, name="%s%d" % key)
             return vals[key]
 
+        def val(name, h, g):
+            if g is None:
+                return both(name, h)[:]
+            return both(name, h)[:, g, :]
+
+        def pair(name, h, g):
+            return both(name, h, 2)[:, g, :, :]
+
+        def row(name, h, g, r):
+            if g is None:
+                return both(name, h, 2)[:, :, r, :]
+            return both(name, h, 2)[:, g, r, :]
+
         def half_z1(h, g):
-            nc.scalar.activation(out=val("z1h", h, g)[:], in_=bank(h, g, 0)[:, 0, :], func=ACT.Copy, scale=0.5)
+            nc.scalar.activation(out=val("z1h", h, g), in_=bank(h, g, 0)[:, 0, :], func=ACT.Copy, scale=0.5)
 
         def half_z2(h, g):
-            nc.scalar.activation(out=val("z2h", h, g)[:], in_=bank(h, g, 1)[:, 0, :], func=ACT.Copy, scale=0.5)
+            nc.scalar.activation(out=val("z2h", h, g), in_=bank(h, g, 1)[:, 0, :], func=ACT.Copy, scale=0.5)
 
         def tanh_z3(h, g):
-            nc.scalar.activation(out=val("t", h, g)[:], in_=bank(h, g, 2)[:, 0, :], func=ACT.Tanh)
+            nc.scalar.activation(out=val("t", h, g), in_=bank(h, g, 2)[:, 0, :], func=ACT.Tanh)
 
         def square_t(h, g):
-            nc.scalar.activation(out=val("tt", h, g)[:], in_=val("t", h, g)[:], func=ACT.Square)
+            nc.scalar.activation(out=val("tt", h, g), in_=val("t", h, g), func=ACT.Square)
 
         def tanh_a(h, g):
-            nc.scalar.activation(out=val("th", h, g)[:], in_=val("sums", h, g, 2)[:, 0, :], func=ACT.Tanh)
+            nc.scalar.activation(out=val("th", h, g), in_=row("sums", h, g, 0), func=ACT.Tanh)
+
+        def gained_gate(h, g):
+            nc.scalar.activation(
+                out=val("gg", h, g), in_=val("th", h, g), func=ACT.Identity,
+                scale=gain[:, g : g + 1], bias=gain[:, g : g + 1],
+            )
 
         def step_a(h, g):
             nc.vector.tensor_tensor(
-                out=val("prods", h, g, 2)[:],
+                out=pair("prods", h, g),
                 in0=bank(h, g, 1)[:],
-                in1=val("z1h", h, g)[:].unsqueeze(1).to_broadcast([P, 2, HALF]),
+                in1=val("z1h", h, g).unsqueeze(1).to_broadcast([P, 2, HALF]),
                 op=ALU.mult,
             )
 
         def step_b(h, g):
-            nc.vector.tensor_tensor(out=val("m1", h, g)[:], in0=bank(h, g, 0)[:, 1, :], in1=val("z2h", h, g)[:], op=ALU.mult)
+            nc.vector.tensor_tensor(out=val("m1", h, g), in0=bank(h, g, 0)[:, 1, :], in1=val("z2h", h, g), op=ALU.mult)
 
         def step_c(h, g):
             nc.vector.scalar_tensor_tensor(
-                out=val("sums", h, g, 2)[:], in0=bank(h, g, 2)[:], scalar=0.5, in1=val("prods", h, g, 2)[:],
+                out=pair("sums", h, g), in0=bank(h, g, 2)[:], scalar=0.5, in1=pair("prods", h, g),
                 op0=ALU.mult, op1=ALU.add,
             )
 
         def step_d(h, g):
             nc.vector.scalar_tensor_tensor(
-                out=val("q", h, g)[:], in0=val("tt", h, g)[:], scalar=1.0, in1=bank(h, g, 2)[:, 1, :],
+                out=val("q", h, g), in0=val("tt", h, g), scalar=1.0, in1=bank(h, g, 2)[:, 1, :],
                 op0=ALU.subtract, op1=ALU.mult,
             )
 
         def step_sum(h, g):
-            nc.vector.tensor_tensor(out=val("b", h, g)[:], in0=val("m1", h, g)[:], in1=val("sums", h, g, 2)[:, 1, :], op=ALU.add)
+            nc.vector.tensor_tensor(out=val("b", h, g), in0=val("m1", h, g), in1=row("sums", h, g, 1), op=ALU.add)
 
         def step_u(h, g):
             nc.vector.scalar_tensor_tensor(
-                out=val("u", h, g)[:], in0=val("th", h, g)[:], scalar=1.0, in1=val("t", h, g)[:],
+                out=val("u", h, g), in0=val("th", h, g), scalar=1.0, in1=val("t", h, g),
                 op0=ALU.subtract, op1=ALU.mult,
             )
 
-        def step_r(h, g):
-            nc.vector.tensor_tensor(out=val("r", h, g)[:], in0=val("b", h, g)[:], in1=val("u", h, g)[:], op=ALU.mult)
+        def step_r(h, g, engine=nc.vector):
+            engine.tensor_tensor(out=val("r", h, g), in0=val("b", h, g), in1=val("u", h, g), op=ALU.mult)
 
-        def step_s(h, g):
-            nc.vector.tensor_tensor(out=val("s", h, g)[:], in0=val("r", h, g)[:], in1=val("q", h, g)[:], op=ALU.add)
+        def step_s(h, g, engine=nc.vector):
+            engine.tensor_tensor(out=val("s", h, g), in0=val("r", h, g), in1=val("q", h, g), op=ALU.add)
 
         def step_w(h, g):
             nc.vector.scalar_tensor_tensor(
-                out=val("w", h, g)[:], in0=val("th", h, g)[:], scalar=1.0, in1=val("s", h, g)[:],
+                out=val("w", h, g), in0=val("th", h, g), scalar=1.0, in1=val("s", h, g),
                 op0=ALU.add, op1=ALU.mult,
             )
 
         def step_y(h, g):
             cols = slice(HALF * h, HALF * (h + 1))
             nc.vector.scalar_tensor_tensor(
-                out=val("y", h, g)[:], in0=val("w", h, g)[:], scalar=gain[:, g : g + 1], in1=base_sb[g][:, cols],
+                out=val("y", h, g), in0=val("w", h, g), scalar=gain[:, g : g + 1], in1=base_sb[h][:, g, :],
                 op0=ALU.mult, op1=ALU.add,
             )
-            nc.sync.dma_start(out=out[g, :, cols], in_=val("y", h, g)[:])
+            nc.sync.dma_start(out=out[g, :, cols], in_=val("y", h, g))
 
         w1_raw = load_rows("w1_raw", w1, 0, M)
         x0_raw = load_rows("x0_raw", x, 0, HALF)
@@ -152,12 +171,13 @@ def tile_rows_tnbilinsig_kernel(tc, x, w1, w2, w3, dx, og, base, out):
         og_sb = sb.tile([P, G, 8], F32, name="og_sb")
         with nc.allow_non_contiguous_dma(reason="one gain a partition"):
             nc.sync.dma_start(out=og_sb[:, :, 0:1], in_=og.rearrange("g m o -> m g o"))
-        base_sb = [sb.tile([P, N], F32, name="base%d" % g) for g in range(G)]
-        for g in range(G):
-            nc.sync.dma_start(out=base_sb[g][:], in_=base[g])
+        base_sb = [sb.tile([P, G, HALF], F32, name="base%d" % h) for h in range(2)]
+        for h in range(2):
+            nc.sync.dma_start(out=base_sb[h][:], in_=base.rearrange("g m n -> m g n")[:, :, HALF * h : HALF * (h + 1)])
         gain = sb.tile([P, G], F32, name="gain")
 
-        w_bf = [rounded("wb%d" % i, M) for i in range(3)]
+        w_bf = [rounded("wb%d" % i, M) for i in range(2)]
+        w_bf.append(sb.tile([P, M, PACK], BF16, name="wb2", tag="late_bf", align_bytes=64))
         interleave(nc.vector.tensor_copy, w_bf[0], 0, w1_raw, 0, M)
         quantize(w_codes[0], w_scales[0], 0, w_bf[0])
         for name, raw, c0 in (("x0", x0_raw, 0), ("dx0", dx0_raw, HALF)):
@@ -176,13 +196,17 @@ def tile_rows_tnbilinsig_kernel(tc, x, w1, w2, w3, dx, og, base, out):
         interleave(nc.vector.tensor_copy, w_bf[2], 0, w3_raw, 0, M)
 
         x1_bf = rounded("x1b", HALF)
-        dx1_bf = rounded("dx1b", HALF)
 
         half_z1(0, 0)
         step_a(0, 0)
         quantize(w_codes[2], w_scales[2], 0, w_bf[2])
         product(0, 0, 2)
         product(0, 1, 2)
+        dx1_bf = sb.tile([P, HALF, PACK], BF16, name="dx1b", tag="late_bf", align_bytes=64)
+        nc.gpsimd.tensor_scalar(
+            out=dx1_bf[:], in0=dx1_raw[:].rearrange("p j c -> p c j"), scalar1=1.0, scalar2=0.0,
+            op0=ALU.mult, op1=ALU.add,
+        )
         interleave(nc.scalar.copy, x1_bf, 0, x1_raw, 0, PIECE)
         half_z2(0, 0)
         half_z1(0, 1)
@@ -194,47 +218,45 @@ def tile_rows_tnbilinsig_kernel(tc, x, w1, w2, w3, dx, og, base, out):
         step_b(0, 1)
         step_c(0, 1)
         quantize(x_codes[1], x_scales[1], 0, x1_bf)
+        quantize(x_codes[1], x_scales[1], HALF, dx1_bf)
+        for g, i in ((0, 0), (0, 1), (1, 0), (1, 1), (0, 2), (1, 2)):
+            product(1, g, i)
         for g in range(G):
             tanh_z3(0, g)
             tanh_a(0, g)
             square_t(0, g)
-        interleave(nc.scalar.copy, dx1_bf, 0, dx1_raw, 0, PIECE)
-        interleave(nc.scalar.copy, dx1_bf, PIECE, dx1_raw, PIECE, PIECE)
-        nc.scalar.activation(out=gain[:], in_=og_sb[:, :, 0], func=ACT.Copy, scale=-0.5)
-        step_sum(0, 0)
-        step_sum(0, 1)
-        step_u(0, 0)
+        step_sum(0, None)
+        step_u(0, None)
+        step_r(0, None, nc.gpsimd)
         step_d(0, 0)
-        step_u(0, 1)
-        step_r(0, 0)
         step_d(0, 1)
-        step_r(0, 1)
-        step_s(0, 0)
-        quantize(x_codes[1], x_scales[1], HALF, dx1_bf)
-        for g, i in ((0, 0), (0, 1), (1, 0), (1, 1), (0, 2), (1, 2)):
-            product(1, g, i)
-        step_s(0, 1)
-        for step in (step_w, step_y):
-            for g in range(G):
-                step(0, g)
-
-        for g in range(G):
-            half_z1(1, g)
-            half_z2(1, g)
-            step_a(1, g)
-            step_b(1, g)
-        for g in range(G):
-            tanh_z3(1, g)
-            step_c(1, g)
+        step_s(0, None, nc.gpsimd)
+        half_z1(1, 0)
+        half_z2(1, 0)
+        step_a(1, 0)
+        step_b(1, 0)
+        half_z1(1, 1)
+        nc.scalar.activation(out=gain[:], in_=og_sb[:, :, 0], func=ACT.Copy, scale=-0.5)
+        gained_gate(0, 0)
+        gained_gate(0, 1)
+        nc.gpsimd.tensor_tensor(out=val("w", 0, None), in0=val("s", 0, None), in1=val("gg", 0, None), op=ALU.mult)
+        step_a(1, 1)
+        half_z2(1, 1)
+        step_c(1, 0)
+        step_b(1, 1)
+        tanh_z3(1, 1)
+        step_c(1, 1)
+        tanh_z3(1, 0)
         square_t(1, 0)
-        tanh_a(1, 0)
         square_t(1, 1)
+        tanh_a(1, 0)
         tanh_a(1, 1)
-        step_sum(1, 0)
-        step_sum(1, 1)
         step_d(1, 0)
-        step_u(1, 0)
         step_d(1, 1)
+        nc.vector.tensor_tensor(out=val("y", 0, None), in0=val("w", 0, None), in1=base_sb[0][:], op=ALU.add)
+        nc.sync.dma_start(out=out.rearrange("g m n -> m g n")[:, :, 0:HALF], in_=val("y", 0, None))
+        step_sum(1, None)
+        step_u(1, 0)
         step_u(1, 1)
         for step in (step_r, step_s, step_w, step_y):
             for g in range(G):

@@ -16,6 +16,15 @@ PACK = 4
 ROWS = D // PACK
 HALF = N // 2
 PIECE = 128
+RUN = 4
+BANKS = 4
+GAIN_PAD = 8
+BOTH = None
+
+PLACES = (
+    {"z1": (0, 0), "tz3": (0, 1), "z2": (1, 0), "z3": (3, 0), "tz2": (2, 0), "tz1": (2, 1)},
+    {"z1": (1, 0), "z3": (1, 1), "z2": (3, 0), "tz3": (3, 1), "tz2": (2, 0), "tz1": (2, 1)},
+)
 
 
 def tile_rows_tnbilinsig_kernel(tc, x, w1, w2, w3, dx, og, base, out):
@@ -28,13 +37,15 @@ def tile_rows_tnbilinsig_kernel(tc, x, w1, w2, w3, dx, og, base, out):
             nc.sync.dma_start(out=raw[:], in_=rows[:, :, c0 : c0 + width])
             return raw
 
-        def interleave(copy, grouped, g0, raw, c0, width):
+        def interleave(copy, grouped, raw, c0):
+            width = grouped.shape[1]
             copy(
-                out=grouped[:, g0 : g0 + width, :].rearrange("p (c i) j -> p c j i", i=4),
-                in_=raw[:, :, c0 : c0 + width].rearrange("p j (c i) -> p c j i", i=4),
+                out=grouped[:].rearrange("p (c i) j -> p c j i", i=RUN),
+                in_=raw[:, :, c0 : c0 + width].rearrange("p j (c i) -> p c j i", i=RUN),
             )
 
-        def quantize(codes, scales, c0, grouped):
+        def quantize(operand, c0, grouped):
+            codes, scales = operand
             width = grouped.shape[1]
             nc.vector.quantize_mx(
                 out=codes[:, c0 : c0 + width].bitcast(FP8X4),
@@ -42,133 +53,143 @@ def tile_rows_tnbilinsig_kernel(tc, x, w1, w2, w3, dx, og, base, out):
                 in_=grouped[:].rearrange("p c j -> p (c j)"),
             )
 
-        def rounded(name, width):
-            return sb.tile([P, width, PACK], BF16, name=name, align_bytes=64)
+        def rounded(name, width, tag=""):
+            return sb.tile([P, width, PACK], BF16, name=name, tag=tag, align_bytes=64)
 
-        w_codes = [sb.tile([P, M], U32, name="wc%d" % i, align_bytes=64) for i in range(3)]
-        w_scales = [sb.tile([P, M], U8, name="ws%d" % i, align_bytes=64) for i in range(3)]
-        x_codes = [sb.tile([P, N], U32, name="xc%d" % h, align_bytes=64) for h in range(2)]
-        x_scales = [sb.tile([P, N], U8, name="xs%d" % h, align_bytes=64) for h in range(2)]
-        banks = [[ps.tile([P, 2, HALF], F32, name="bank%d_%d" % (g, b)) for b in range(4)] for g in range(G)]
+        def mx_operand(name, width):
+            codes = sb.tile([P, width], U32, name=name + "_codes", align_bytes=64)
+            scales = sb.tile([P, width], U8, name=name + "_scales", align_bytes=64)
+            return codes, scales
 
-        def bank(h, g, i):
-            return banks[g][(3 * h + i) % 4]
+        w_mx = [mx_operand("w%d" % i, M) for i in range(3)]
+        x_mx = [mx_operand("x%d" % h, HALF) for h in range(2)]
+        dx_mx = [mx_operand("dx%d" % h, HALF) for h in range(2)]
+        banks = [[ps.tile([P, 2, HALF], F32, name="bank%d_%d" % (g, b)) for b in range(BANKS)] for g in range(G)]
 
-        def product(h, g, i):
+        def sums(name, h, g):
+            b, side = PLACES[h][name]
+            return banks[g][b][:, side, :]
+
+        def product(name, h, g):
             rows = slice(ROWS * g, ROWS * (g + 1))
-            nc.tensor.matmul_mx(
-                out=bank(h, g, i)[:].rearrange("p a n -> p (a n)"),
-                lhsT=w_codes[i][rows, :].bitcast(FP8X4),
-                lhsT_scale=w_scales[i][rows, :],
-                rhs=x_codes[h][rows, :].bitcast(FP8X4),
-                rhs_scale=x_scales[h][rows, :],
-                start=True,
-                stop=True,
-            )
+            w_codes, w_scales = w_mx[int(name[-1]) - 1]
+            codes, scales = (dx_mx if name.startswith("t") else x_mx)[h]
+            for c0 in range(0, HALF, PIECE):
+                cols = slice(c0, c0 + PIECE)
+                nc.tensor.matmul_mx(
+                    out=sums(name, h, g)[:, cols],
+                    lhsT=w_codes[rows, :].bitcast(FP8X4),
+                    lhsT_scale=w_scales[rows, :],
+                    rhs=codes[rows, cols].bitcast(FP8X4),
+                    rhs_scale=scales[rows, cols],
+                    start=True,
+                    stop=True,
+                )
 
-        vals = {}
+        def products(names, h):
+            for g in range(G):
+                for name in names:
+                    product(name, h, g)
 
-        def both(name, h, rows=1):
-            key = (name, h)
-            if key not in vals:
-                shape = [P, G, HALF] if rows == 1 else [P, G, rows, HALF]
-                vals[key] = sb.tile(shape, F32, name="%s%d" % key)
-            return vals[key]
+        tiles = {}
+
+        def values(name, h, shape):
+            if (name, h) not in tiles:
+                tiles[(name, h)] = sb.tile(shape, F32, name="%s%d" % (name, h))
+            return tiles[(name, h)]
 
         def val(name, h, g):
-            if g is None:
-                return both(name, h)[:]
-            return both(name, h)[:, g, :]
+            tile = values(name, h, [P, G, HALF])
+            return tile[:] if g is BOTH else tile[:, g, :]
 
         def pair(name, h, g):
-            return both(name, h, 2)[:, g, :, :]
+            return values(name, h, [P, G, 2, HALF])[:, g, :, :]
 
-        def row(name, h, g, r):
-            if g is None:
-                return both(name, h, 2)[:, :, r, :]
-            return both(name, h, 2)[:, g, r, :]
+        def pair_side(name, h, g, side):
+            tile = values(name, h, [P, G, 2, HALF])
+            return tile[:, :, side, :] if g is BOTH else tile[:, g, side, :]
 
         def half_z1(h, g):
-            nc.scalar.activation(out=val("z1h", h, g), in_=bank(h, g, 0)[:, 0, :], func=ACT.Copy, scale=0.5)
+            nc.scalar.activation(out=pair_side("zh", h, g, 0), in_=sums("z1", h, g), func=ACT.Copy, scale=0.5)
 
         def half_z2(h, g):
-            nc.scalar.activation(out=val("z2h", h, g), in_=bank(h, g, 1)[:, 0, :], func=ACT.Copy, scale=0.5)
+            nc.scalar.activation(out=pair_side("zh", h, g, 1), in_=sums("z2", h, g), func=ACT.Copy, scale=0.5)
 
         def tanh_z3(h, g):
-            nc.scalar.activation(out=val("t", h, g), in_=bank(h, g, 2)[:, 0, :], func=ACT.Tanh)
+            nc.scalar.activation(out=val("t", h, g), in_=sums("z3", h, g), func=ACT.Tanh)
 
-        def square_t(h, g):
-            nc.scalar.activation(out=val("tt", h, g), in_=val("t", h, g), func=ACT.Square)
+        def square_t(h):
+            nc.scalar.activation(out=val("tt", h, BOTH), in_=val("t", h, BOTH), func=ACT.Square)
 
-        def tanh_a(h, g):
-            nc.scalar.activation(out=val("th", h, g), in_=row("sums", h, g, 0), func=ACT.Tanh)
+        def tanh_a(h):
+            nc.scalar.activation(out=val("th", h, BOTH), in_=val("a", h, BOTH), func=ACT.Tanh)
 
-        def gained_gate(h, g):
-            nc.scalar.activation(
-                out=val("gg", h, g), in_=val("th", h, g), func=ACT.Identity,
-                scale=gain[:, g : g + 1], bias=gain[:, g : g + 1],
-            )
+        def step_p(h, g):
+            nc.vector.tensor_tensor(out=val("p", h, g), in0=sums("z2", h, g), in1=pair_side("zh", h, g, 0), op=ALU.mult)
 
         def step_a(h, g):
-            nc.vector.tensor_tensor(
-                out=pair("prods", h, g),
-                in0=bank(h, g, 1)[:],
-                in1=val("z1h", h, g).unsqueeze(1).to_broadcast([P, 2, HALF]),
-                op=ALU.mult,
+            nc.vector.scalar_tensor_tensor(
+                out=val("a", h, g), in0=sums("z3", h, g), scalar=0.5, in1=val("p", h, g), op0=ALU.mult, op1=ALU.add,
             )
 
-        def step_b(h, g):
-            nc.vector.tensor_tensor(out=val("m1", h, g), in0=bank(h, g, 0)[:, 1, :], in1=val("z2h", h, g), op=ALU.mult)
+        def step_m(h, g):
+            nc.vector.tensor_tensor(
+                out=pair("m", h, g), in0=banks[g][PLACES[h]["tz2"][0]][:], in1=pair("zh", h, g), op=ALU.mult,
+            )
 
-        def step_c(h, g):
+        def step_n(h, g):
             nc.vector.scalar_tensor_tensor(
-                out=pair("sums", h, g), in0=bank(h, g, 2)[:], scalar=0.5, in1=pair("prods", h, g),
+                out=val("n", h, g), in0=sums("tz3", h, g), scalar=0.5, in1=pair_side("m", h, g, 0),
                 op0=ALU.mult, op1=ALU.add,
             )
 
-        def step_d(h, g):
+        def step_q(h, g):
             nc.vector.scalar_tensor_tensor(
-                out=val("q", h, g), in0=val("tt", h, g), scalar=1.0, in1=bank(h, g, 2)[:, 1, :],
+                out=val("q", h, g), in0=val("tt", h, g), scalar=1.0, in1=sums("tz3", h, g),
                 op0=ALU.subtract, op1=ALU.mult,
             )
 
-        def step_sum(h, g):
-            nc.vector.tensor_tensor(out=val("b", h, g), in0=val("m1", h, g), in1=row("sums", h, g, 1), op=ALU.add)
+        def step_b(h):
+            nc.vector.tensor_tensor(
+                out=val("b", h, BOTH), in0=val("n", h, BOTH), in1=pair_side("m", h, BOTH, 1), op=ALU.add,
+            )
 
-        def step_u(h, g):
+        def step_u(h):
             nc.vector.scalar_tensor_tensor(
-                out=val("u", h, g), in0=val("th", h, g), scalar=1.0, in1=val("t", h, g),
+                out=val("u", h, BOTH), in0=val("th", h, BOTH), scalar=1.0, in1=val("t", h, BOTH),
                 op0=ALU.subtract, op1=ALU.mult,
             )
 
-        def step_r(h, g, engine=nc.vector):
+        def step_r(h, g, engine):
             engine.tensor_tensor(out=val("r", h, g), in0=val("b", h, g), in1=val("u", h, g), op=ALU.mult)
 
-        def step_s(h, g, engine=nc.vector):
+        def step_s(h, g, engine):
             engine.tensor_tensor(out=val("s", h, g), in0=val("r", h, g), in1=val("q", h, g), op=ALU.add)
 
         def step_w(h, g):
             nc.vector.scalar_tensor_tensor(
-                out=val("w", h, g), in0=val("th", h, g), scalar=1.0, in1=val("s", h, g),
-                op0=ALU.add, op1=ALU.mult,
+                out=val("w", h, g), in0=val("th", h, g), scalar=1.0, in1=val("s", h, g), op0=ALU.add, op1=ALU.mult,
             )
 
-        def step_y(h, g):
-            cols = slice(HALF * h, HALF * (h + 1))
+        def step_out(h, g):
             nc.vector.scalar_tensor_tensor(
                 out=val("y", h, g), in0=val("w", h, g), scalar=gain[:, g : g + 1], in1=base_sb[h][:, g, :],
                 op0=ALU.mult, op1=ALU.add,
             )
-            nc.sync.dma_start(out=out[g, :, cols], in_=val("y", h, g))
+            nc.sync.dma_start(out=out[g, :, HALF * h : HALF * (h + 1)], in_=val("y", h, g))
+
+        def per_group(step, h, *engine):
+            for g in range(G):
+                step(h, g, *engine)
 
         w1_raw = load_rows("w1_raw", w1, 0, M)
         x0_raw = load_rows("x0_raw", x, 0, HALF)
-        dx0_raw = load_rows("dx0_raw", dx, 0, HALF)
         w2_raw = load_rows("w2_raw", w2, 0, M)
         w3_raw = load_rows("w3_raw", w3, 0, M)
+        dx0_raw = load_rows("dx0_raw", dx, 0, HALF)
         x1_raw = load_rows("x1_raw", x, HALF, HALF)
         dx1_raw = load_rows("dx1_raw", dx, HALF, HALF)
-        og_sb = sb.tile([P, G, 8], F32, name="og_sb")
+        og_sb = sb.tile([P, G, GAIN_PAD], F32, name="og_sb")
         with nc.allow_non_contiguous_dma(reason="one gain a partition"):
             nc.sync.dma_start(out=og_sb[:, :, 0:1], in_=og.rearrange("g m o -> m g o"))
         base_sb = [sb.tile([P, G, HALF], F32, name="base%d" % h) for h in range(2)]
@@ -176,88 +197,81 @@ def tile_rows_tnbilinsig_kernel(tc, x, w1, w2, w3, dx, og, base, out):
             nc.sync.dma_start(out=base_sb[h][:], in_=base.rearrange("g m n -> m g n")[:, :, HALF * h : HALF * (h + 1)])
         gain = sb.tile([P, G], F32, name="gain")
 
-        w_bf = [rounded("wb%d" % i, M) for i in range(2)]
-        w_bf.append(sb.tile([P, M, PACK], BF16, name="wb2", tag="late_bf", align_bytes=64))
-        interleave(nc.vector.tensor_copy, w_bf[0], 0, w1_raw, 0, M)
-        quantize(w_codes[0], w_scales[0], 0, w_bf[0])
-        for name, raw, c0 in (("x0", x0_raw, 0), ("dx0", dx0_raw, HALF)):
-            lo = rounded(name + "lo", PIECE)
-            hi = rounded(name + "hi", PIECE)
-            interleave(nc.vector.tensor_copy, lo, 0, raw, 0, PIECE)
-            interleave(nc.scalar.copy, hi, 0, raw, PIECE, PIECE)
-            quantize(x_codes[0], x_scales[0], c0, lo)
-            quantize(x_codes[0], x_scales[0], c0 + PIECE, hi)
-        product(0, 0, 0)
-        interleave(nc.scalar.copy, w_bf[1], 0, w2_raw, 0, M)
-        quantize(w_codes[1], w_scales[1], 0, w_bf[1])
-        product(0, 0, 1)
-        product(0, 1, 0)
-        product(0, 1, 1)
-        interleave(nc.vector.tensor_copy, w_bf[2], 0, w3_raw, 0, M)
+        w_bf = [rounded("wb%d" % i, M) for i in range(3)]
+        x0_lo = rounded("x0lo", PIECE)
+        x0_hi = rounded("x0hi", PIECE)
+        dx0_lo = rounded("dx0lo", PIECE)
+        dx0_hi = rounded("dx0hi", PIECE, tag="late_bf")
+        dx1_bf = rounded("dx1b", HALF)
 
-        x1_bf = rounded("x1b", HALF)
-
+        interleave(nc.vector.tensor_copy, w_bf[0], w1_raw, 0)
+        quantize(w_mx[0], 0, w_bf[0])
+        interleave(nc.vector.tensor_copy, x0_lo, x0_raw, 0)
+        interleave(nc.scalar.copy, x0_hi, x0_raw, PIECE)
+        interleave(nc.vector.tensor_copy, w_bf[1], w2_raw, 0)
+        quantize(x_mx[0], 0, x0_lo)
+        quantize(x_mx[0], PIECE, x0_hi)
+        quantize(w_mx[1], 0, w_bf[1])
+        interleave(nc.scalar.copy, w_bf[2], w3_raw, 0)
+        quantize(w_mx[2], 0, w_bf[2])
+        products(("z1", "z2"), 0)
+        products(("z3",), 0)
         half_z1(0, 0)
-        step_a(0, 0)
-        quantize(w_codes[2], w_scales[2], 0, w_bf[2])
-        product(0, 0, 2)
-        product(0, 1, 2)
-        dx1_bf = sb.tile([P, HALF, PACK], BF16, name="dx1b", tag="late_bf", align_bytes=64)
+        interleave(nc.vector.tensor_copy, dx0_lo, dx0_raw, 0)
+        step_p(0, 0)
+        interleave(nc.scalar.copy, dx0_hi, dx0_raw, PIECE)
+        half_z1(0, 1)
+        quantize(dx_mx[0], 0, dx0_lo)
+        quantize(dx_mx[0], PIECE, dx0_hi)
+
+        x1_bf = rounded("x1_bf", HALF, tag="late_bf")
         nc.gpsimd.tensor_scalar(
-            out=dx1_bf[:], in0=dx1_raw[:].rearrange("p j c -> p c j"), scalar1=1.0, scalar2=0.0,
+            out=x1_bf[:], in0=x1_raw[:].rearrange("p j c -> p c j"), scalar1=1.0, scalar2=0.0,
             op0=ALU.mult, op1=ALU.add,
         )
-        interleave(nc.scalar.copy, x1_bf, 0, x1_raw, 0, PIECE)
-        half_z2(0, 0)
-        half_z1(0, 1)
-        step_b(0, 0)
-        step_a(0, 1)
-        interleave(nc.scalar.copy, x1_bf, PIECE, x1_raw, PIECE, PIECE)
-        half_z2(0, 1)
-        step_c(0, 0)
-        step_b(0, 1)
-        step_c(0, 1)
-        quantize(x_codes[1], x_scales[1], 0, x1_bf)
-        quantize(x_codes[1], x_scales[1], HALF, dx1_bf)
-        for g, i in ((0, 0), (0, 1), (1, 0), (1, 1), (0, 2), (1, 2)):
-            product(1, g, i)
-        for g in range(G):
-            tanh_z3(0, g)
-            tanh_a(0, g)
-            square_t(0, g)
-        step_sum(0, None)
-        step_u(0, None)
-        step_r(0, None, nc.gpsimd)
-        step_d(0, 0)
-        step_d(0, 1)
-        step_s(0, None, nc.gpsimd)
-        half_z1(1, 0)
-        half_z2(1, 0)
-        step_a(1, 0)
-        step_b(1, 0)
-        half_z1(1, 1)
+        step_p(0, 1)
+        per_group(half_z2, 0)
+        per_group(step_a, 0)
+        products(("tz2", "tz1"), 0)
+        products(("tz3",), 0)
+        per_group(tanh_z3, 0)
+        tanh_a(0)
+        per_group(step_m, 0)
+        per_group(step_n, 0)
+        interleave(nc.scalar.copy, dx1_bf, dx1_raw, 0)
+        square_t(0)
+
+        quantize(x_mx[1], 0, x1_bf)
+        products(("z1", "z2"), 1)
+        per_group(half_z1, 1)
+        products(("z3",), 1)
+        step_u(0)
+        quantize(dx_mx[1], 0, dx1_bf)
+        products(("tz2", "tz1"), 1)
+        step_b(0)
+
+        step_r(0, BOTH, nc.gpsimd)
+        step_q(0, 0)
+        per_group(step_p, 1)
+        step_q(0, 1)
+        step_s(0, BOTH, nc.gpsimd)
+        per_group(half_z2, 1)
+        products(("tz3",), 1)
+        per_group(step_a, 1)
+        per_group(tanh_z3, 1)
         nc.scalar.activation(out=gain[:], in_=og_sb[:, :, 0], func=ACT.Copy, scale=-0.5)
-        gained_gate(0, 0)
-        gained_gate(0, 1)
-        nc.gpsimd.tensor_tensor(out=val("w", 0, None), in0=val("s", 0, None), in1=val("gg", 0, None), op=ALU.mult)
-        step_a(1, 1)
-        half_z2(1, 1)
-        step_c(1, 0)
-        step_b(1, 1)
-        tanh_z3(1, 1)
-        step_c(1, 1)
-        tanh_z3(1, 0)
-        square_t(1, 0)
-        square_t(1, 1)
-        tanh_a(1, 0)
-        tanh_a(1, 1)
-        step_d(1, 0)
-        step_d(1, 1)
-        nc.vector.tensor_tensor(out=val("y", 0, None), in0=val("w", 0, None), in1=base_sb[0][:], op=ALU.add)
-        nc.sync.dma_start(out=out.rearrange("g m n -> m g n")[:, :, 0:HALF], in_=val("y", 0, None))
-        step_sum(1, None)
-        step_u(1, 0)
-        step_u(1, 1)
-        for step in (step_r, step_s, step_w, step_y):
-            for g in range(G):
-                step(1, g)
+        square_t(1)
+        tanh_a(1)
+        per_group(step_m, 1)
+        per_group(step_n, 1)
+        per_group(step_q, 1)
+
+        step_b(1)
+        step_u(1)
+        step_w(0, BOTH)
+        per_group(step_r, 1, nc.vector)
+        step_out(0, 0)
+        per_group(step_s, 1, nc.vector)
+        step_out(0, 1)
+        per_group(step_w, 1)
+        per_group(step_out, 1)

import concourse.mybir as mybir

G, D, M, N = 2, 256, 128, 512
FLOPS = 6 * 2 * G * D * M * N

F32 = mybir.dt.float32
BF16 = mybir.dt.bfloat16
U32 = mybir.dt.uint32
U8 = mybir.dt.uint8
FP8X4 = mybir.dt.float8_e4m3fn_x4
ALU = mybir.AluOpType
ACT = mybir.ActivationFunctionType

P = 128
PACK = 4
ROWS = D // PACK
HALF = N // 2
PIECE = 128
RUN = 4
BANKS = 4
GAIN_PAD = 8
BOTH = None

PLACES = (
    {"z1": (0, 0), "tz3": (0, 1), "z2": (1, 0), "z3": (3, 0), "tz2": (2, 0), "tz1": (2, 1)},
    {"z1": (1, 0), "z3": (1, 1), "z2": (3, 0), "tz3": (3, 1), "tz2": (2, 0), "tz1": (2, 1)},
)


def tile_rows_tnbilinsig_kernel(tc, x, w1, w2, w3, dx, og, base, out):
    nc = tc.nc
    with tc.tile_pool(name="sbuf", bufs=1) as sb, tc.psum_pool(name="psum", bufs=1) as ps, tc.manual_schedule():

        def load_rows(name, src, c0, width):
            raw = sb.tile([P, PACK, width], F32, name=name)
            rows = src.rearrange("g (p j) n -> (g p) j n", j=PACK)
            nc.sync.dma_start(out=raw[:], in_=rows[:, :, c0 : c0 + width])
            return raw

        def interleave(copy, grouped, raw, c0):
            width = grouped.shape[1]
            copy(
                out=grouped[:].rearrange("p (c i) j -> p c j i", i=RUN),
                in_=raw[:, :, c0 : c0 + width].rearrange("p j (c i) -> p c j i", i=RUN),
            )

        def quantize(operand, c0, grouped):
            codes, scales = operand
            width = grouped.shape[1]
            nc.vector.quantize_mx(
                out=codes[:, c0 : c0 + width].bitcast(FP8X4),
                scales=scales[:, c0 : c0 + width],
                in_=grouped[:].rearrange("p c j -> p (c j)"),
            )

        def rounded(name, width, tag=""):
            return sb.tile([P, width, PACK], BF16, name=name, tag=tag, align_bytes=64)

        def mx_operand(name, width):
            codes = sb.tile([P, width], U32, name=name + "_codes", align_bytes=64)
            scales = sb.tile([P, width], U8, name=name + "_scales", align_bytes=64)
            return codes, scales

        w_mx = [mx_operand("w%d" % i, M) for i in range(3)]
        x_mx = [mx_operand("x%d" % h, HALF) for h in range(2)]
        dx_mx = [mx_operand("dx%d" % h, HALF) for h in range(2)]
        banks = [[ps.tile([P, 2, HALF], F32, name="bank%d_%d" % (g, b)) for b in range(BANKS)] for g in range(G)]

        def sums(name, h, g):
            b, side = PLACES[h][name]
            return banks[g][b][:, side, :]

        def product(name, h, g):
            rows = slice(ROWS * g, ROWS * (g + 1))
            w_codes, w_scales = w_mx[int(name[-1]) - 1]
            codes, scales = (dx_mx if name.startswith("t") else x_mx)[h]
            for c0 in range(0, HALF, PIECE):
                cols = slice(c0, c0 + PIECE)
                nc.tensor.matmul_mx(
                    out=sums(name, h, g)[:, cols],
                    lhsT=w_codes[rows, :].bitcast(FP8X4),
                    lhsT_scale=w_scales[rows, :],
                    rhs=codes[rows, cols].bitcast(FP8X4),
                    rhs_scale=scales[rows, cols],
                    start=True,
                    stop=True,
                )

        def products(names, h):
            for g in range(G):
                for name in names:
                    product(name, h, g)

        tiles = {}

        def values(name, h, shape):
            if (name, h) not in tiles:
                tiles[(name, h)] = sb.tile(shape, F32, name="%s%d" % (name, h))
            return tiles[(name, h)]

        def val(name, h, g):
            tile = values(name, h, [P, G, HALF])
            return tile[:] if g is BOTH else tile[:, g, :]

        def pair(name, h, g):
            return values(name, h, [P, G, 2, HALF])[:, g, :, :]

        def pair_side(name, h, g, side):
            tile = values(name, h, [P, G, 2, HALF])
            return tile[:, :, side, :] if g is BOTH else tile[:, g, side, :]

        def half_z1(h, g):
            nc.scalar.activation(out=pair_side("zh", h, g, 0), in_=sums("z1", h, g), func=ACT.Copy, scale=0.5)

        def half_z2(h, g):
            nc.scalar.activation(out=pair_side("zh", h, g, 1), in_=sums("z2", h, g), func=ACT.Copy, scale=0.5)

        def tanh_z3(h, g):
            nc.scalar.activation(out=val("t", h, g), in_=sums("z3", h, g), func=ACT.Tanh)

        def square_t(h):
            nc.scalar.activation(out=val("tt", h, BOTH), in_=val("t", h, BOTH), func=ACT.Square)

        def tanh_a(h):
            nc.scalar.activation(out=val("th", h, BOTH), in_=val("a", h, BOTH), func=ACT.Tanh)

        def step_p(h, g):
            nc.vector.tensor_tensor(out=val("p", h, g), in0=sums("z2", h, g), in1=pair_side("zh", h, g, 0), op=ALU.mult)

        def step_a(h, g):
            nc.vector.scalar_tensor_tensor(
                out=val("a", h, g), in0=sums("z3", h, g), scalar=0.5, in1=val("p", h, g), op0=ALU.mult, op1=ALU.add,
            )

        def step_m(h, g):
            nc.vector.tensor_tensor(
                out=pair("m", h, g), in0=banks[g][PLACES[h]["tz2"][0]][:], in1=pair("zh", h, g), op=ALU.mult,
            )

        def step_n(h, g):
            nc.vector.scalar_tensor_tensor(
                out=val("n", h, g), in0=sums("tz3", h, g), scalar=0.5, in1=pair_side("m", h, g, 0),
                op0=ALU.mult, op1=ALU.add,
            )

        def step_q(h, g):
            nc.vector.scalar_tensor_tensor(
                out=val("q", h, g), in0=val("tt", h, g), scalar=1.0, in1=sums("tz3", h, g),
                op0=ALU.subtract, op1=ALU.mult,
            )

        def step_b(h):
            nc.vector.tensor_tensor(
                out=val("b", h, BOTH), in0=val("n", h, BOTH), in1=pair_side("m", h, BOTH, 1), op=ALU.add,
            )

        def step_u(h):
            nc.vector.scalar_tensor_tensor(
                out=val("u", h, BOTH), in0=val("th", h, BOTH), scalar=1.0, in1=val("t", h, BOTH),
                op0=ALU.subtract, op1=ALU.mult,
            )

        def step_r(h, g, engine):
            engine.tensor_tensor(out=val("r", h, g), in0=val("b", h, g), in1=val("u", h, g), op=ALU.mult)

        def step_s(h, g, engine):
            engine.tensor_tensor(out=val("s", h, g), in0=val("r", h, g), in1=val("q", h, g), op=ALU.add)

        def step_w(h, g):
            nc.vector.scalar_tensor_tensor(
                out=val("w", h, g), in0=val("th", h, g), scalar=1.0, in1=val("s", h, g), op0=ALU.add, op1=ALU.mult,
            )

        def step_out(h, g):
            nc.vector.scalar_tensor_tensor(
                out=val("y", h, g), in0=val("w", h, g), scalar=gain[:, g : g + 1], in1=base_sb[h][:, g, :],
                op0=ALU.mult, op1=ALU.add,
            )
            nc.sync.dma_start(out=out[g, :, HALF * h : HALF * (h + 1)], in_=val("y", h, g))

        def per_group(step, h, *engine):
            for g in range(G):
                step(h, g, *engine)

        w1_raw = load_rows("w1_raw", w1, 0, M)
        x0_raw = load_rows("x0_raw", x, 0, HALF)
        w2_raw = load_rows("w2_raw", w2, 0, M)
        w3_raw = load_rows("w3_raw", w3, 0, M)
        dx0_raw = load_rows("dx0_raw", dx, 0, HALF)
        x1_raw = load_rows("x1_raw", x, HALF, HALF)
        dx1_raw = load_rows("dx1_raw", dx, HALF, HALF)
        og_sb = sb.tile([P, G, GAIN_PAD], F32, name="og_sb")
        with nc.allow_non_contiguous_dma(reason="one gain a partition"):
            nc.sync.dma_start(out=og_sb[:, :, 0:1], in_=og.rearrange("g m o -> m g o"))
        base_sb = [sb.tile([P, G, HALF], F32, name="base%d" % h) for h in range(2)]
        for h in range(2):
            nc.sync.dma_start(out=base_sb[h][:], in_=base.rearrange("g m n -> m g n")[:, :, HALF * h : HALF * (h + 1)])
        gain = sb.tile([P, G], F32, name="gain")

        w_bf = [rounded("wb%d" % i, M) for i in range(3)]
        x0_lo = rounded("x0lo", PIECE)
        x0_hi = rounded("x0hi", PIECE)
        dx0_lo = rounded("dx0lo", PIECE)
        dx0_hi = rounded("dx0hi", PIECE, tag="late_bf")
        dx1_bf = rounded("dx1b", HALF)

        interleave(nc.vector.tensor_copy, w_bf[0], w1_raw, 0)
        quantize(w_mx[0], 0, w_bf[0])
        interleave(nc.vector.tensor_copy, x0_lo, x0_raw, 0)
        interleave(nc.scalar.copy, x0_hi, x0_raw, PIECE)
        interleave(nc.vector.tensor_copy, w_bf[1], w2_raw, 0)
        quantize(x_mx[0], 0, x0_lo)
        quantize(x_mx[0], PIECE, x0_hi)
        quantize(w_mx[1], 0, w_bf[1])
        interleave(nc.scalar.copy, w_bf[2], w3_raw, 0)
        quantize(w_mx[2], 0, w_bf[2])
        products(("z1", "z2"), 0)
        products(("z3",), 0)
        half_z1(0, 0)
        interleave(nc.vector.tensor_copy, dx0_lo, dx0_raw, 0)
        step_p(0, 0)
        interleave(nc.scalar.copy, dx0_hi, dx0_raw, PIECE)
        half_z1(0, 1)
        quantize(dx_mx[0], 0, dx0_lo)
        quantize(dx_mx[0], PIECE, dx0_hi)

        x1_bf = rounded("x1_bf", HALF, tag="late_bf")
        nc.gpsimd.tensor_scalar(
            out=x1_bf[:], in0=x1_raw[:].rearrange("p j c -> p c j"), scalar1=1.0, scalar2=0.0,
            op0=ALU.mult, op1=ALU.add,
        )
        step_p(0, 1)
        per_group(half_z2, 0)
        per_group(step_a, 0)
        products(("tz2", "tz1"), 0)
        products(("tz3",), 0)
        per_group(tanh_z3, 0)
        tanh_a(0)
        per_group(step_m, 0)
        per_group(step_n, 0)
        interleave(nc.scalar.copy, dx1_bf, dx1_raw, 0)
        square_t(0)

        quantize(x_mx[1], 0, x1_bf)
        products(("z1", "z2"), 1)
        per_group(half_z1, 1)
        products(("z3",), 1)
        step_u(0)
        quantize(dx_mx[1], 0, dx1_bf)
        products(("tz2", "tz1"), 1)
        step_b(0)

        step_r(0, BOTH, nc.gpsimd)
        step_q(0, 0)
        per_group(step_p, 1)
        step_q(0, 1)
        step_s(0, BOTH, nc.gpsimd)
        per_group(half_z2, 1)
        products(("tz3",), 1)
        per_group(step_a, 1)
        per_group(tanh_z3, 1)
        nc.scalar.activation(out=gain[:], in_=og_sb[:, :, 0], func=ACT.Copy, scale=-0.5)
        square_t(1)
        tanh_a(1)
        per_group(step_m, 1)
        per_group(step_n, 1)
        per_group(step_q, 1)

        step_b(1)
        step_u(1)
        step_w(0, BOTH)
        per_group(step_r, 1, nc.vector)
        step_out(0, 0)
        per_group(step_s, 1, nc.vector)
        step_out(0, 1)
        per_group(step_w, 1)
        per_group(step_out, 1)
